import numpy as np
import ml_dtypes


def mxq(x, axis, fmt="e4m3"):
    dtype, down = {"e4m3": (ml_dtypes.float8_e4m3fn, 7), "e5m2": (ml_dtypes.float8_e5m2, 14)}[fmt]
    v = np.moveaxis(np.asarray(x, np.float32).astype(ml_dtypes.bfloat16).astype(np.float64), axis, -1)
    blocks = v.reshape(v.shape[:-1] + (-1, 32))
    amax = np.abs(blocks).max(-1, keepdims=True)
    byte = np.maximum(np.where(amax > 0, np.frexp(amax)[1] - 1 + 127, 0) - down, 1)
    scale = np.exp2(byte - 127.0)
    codes = (blocks / scale).astype(np.float32).astype(dtype).astype(np.float64)
    return np.moveaxis((codes * scale).reshape(v.shape), -1, axis)


WIDE = False


def mx_kscale(k):
    if not WIDE:
        return np.ones(k)
    levels = np.array([10, -10, 5, -5, 0])
    if k % 512:
        return np.exp2(np.random.permutation(np.resize(levels, k // 32))).repeat(32)
    a = np.empty((k // 512, 16))
    for p in range(k // 512):
        a[p, :8] = np.random.permutation(np.resize(levels, 8))
        for g in range(8):
            far = levels[np.abs(levels - a[p, g]) >= 10]
            a[p, g + 8] = far[np.random.randint(len(far))]
    return np.exp2(a.ravel()).repeat(32)


def f64(x):
    return np.asarray(x).astype(np.float64)


def striped(idx):
    return np.tile(np.asarray(idx).reshape(-1, 16).T, (8, 1)).astype(np.uint16)


def unstriped(offs):
    return offs[:16].T.reshape(-1).astype(np.int64)


G, T, D, H = 512, 2048, 512, 512


def setup_inputs():
    n = np.random.standard_normal
    s = mx_kscale(D)[:, None]
    u = mx_kscale(H)[:, None]
    return {
        "xT": (n((D, T)) * s).astype(np.float32),
        "w1": (n((D, H)) / np.sqrt(D) / s * u[:, 0]).astype(np.float32),
        "w2": (n((H, D)) / np.sqrt(H) / u * s[:, 0]).astype(np.float32),
        "offs": striped(np.random.permutation(T)[:G]),
    }


def reference(xT, w1, w2, offs):
    x = f64(xT)
    idx = unstriped(offs)
    a = mxq(f64(w1), 0, "e4m3").T @ mxq(x[:, idx], 0, "e4m3")
    h = np.maximum(a, 0.0)
    y = x[:, idx] + (mxq(f64(w2), 0, "e4m3").T @ mxq(h, 0, "e4m3"))
    out = x.copy()
    out[:, idx] = y
    return out

@@ -1,0 +1,133 @@
+import concourse.mybir as mybir
+
+FLOPS = 2 * 2 * 512 * 512 * 512
+
+F32 = mybir.dt.float32
+BF16 = mybir.dt.bfloat16
+U32 = mybir.dt.uint32
+U16 = mybir.dt.uint16
+U8 = mybir.dt.uint8
+FP8X4 = mybir.dt.float8_e4m3fn_x4
+ADD = mybir.AluOpType.add
+RELU = mybir.ActivationFunctionType.Relu
+
+P = 128
+T = 2048
+D = 512
+H = 512
+G = 512
+X4 = 4
+HALF = G // 2
+CHUNK = 128
+
+
+def tile_attend_mod_relu_kernel(tc, xT, w1, w2, offs, out):
+    nc = tc.nc
+    with (
+        tc.tile_pool(name="lists", bufs=1) as lists,
+        tc.tile_pool(name="keep", bufs=1) as keep,
+        tc.psum_pool(name="psum", bufs=1) as psum,
+    ):
+        offsets = lists.tile([P, G // 16], U16, name="offsets")
+        nc.sync.dma_start(offsets[:], offs)
+
+        x_rows = xT.rearrange("(p t) n -> t p n", t=X4)
+        out_rows = out.rearrange("(p t) n -> t p n", t=X4)
+
+        w1_raw = keep.tile([P, X4, H], F32, name="w1_raw")
+        w2_raw = keep.tile([P, X4, D], F32, name="w2_raw")
+        planes = [keep.tile([P, T], F32, name=f"plane{t}") for t in range(X4)]
+
+        nc.sync.dma_start(out=w1_raw[:], in_=w1.rearrange("(p j) c -> p j c", j=X4))
+        nc.sync.dma_start(out=planes[0][:], in_=x_rows[0])
+        nc.sync.dma_start(out=w2_raw[:], in_=w2.rearrange("(p j) c -> p j c", j=X4))
+        for t in range(1, X4):
+            nc.sync.dma_start(out=planes[t][:], in_=x_rows[t])
+
+        picked = keep.tile([P, X4, G], F32, name="picked")
+        x_grouped = keep.tile([P, G, X4], BF16, name="x_grouped", align_bytes=64)
+
+        def group_weights(raw, name):
+            grouped = keep.tile([P, X4 * 512], BF16, name=name + "_grouped", align_bytes=64)
+            nc.scalar.copy(
+                out=grouped[:].rearrange("p (t m j) -> p t m j", t=X4, j=X4),
+                in_=raw[:].rearrange("p j (m t) -> p t m j", t=X4),
+            )
+            return grouped
+
+        def quantize(grouped, width, name):
+            codes = keep.tile([P, width], U32, name=name + "_codes", align_bytes=64)
+            scales = keep.tile([P, width], U8, name=name + "_scales", align_bytes=64)
+            nc.vector.quantize_mx(out=codes[:].bitcast(FP8X4), scales=scales[:], in_=grouped)
+            return codes, scales
+
+        def early_plane(t):
+            nc.vector.tensor_copy(picked[:, t, :], planes[t][:].indirect(offsets[:]))
+            nc.vector.tensor_copy(x_grouped[:, :, t], picked[:, t, :])
+
+        w1_grouped = group_weights(w1_raw, "w1")
+        early_plane(0)
+        w1_q = quantize(w1_grouped[:], H, "w1")
+        w2_grouped = group_weights(w2_raw, "w2")
+        early_plane(1)
+        early_plane(2)
+        w2_q = quantize(w2_grouped[:], D, "w2")
+
+        half_offsets = [offsets[:, u * (HALF // 16) : (u + 1) * (HALF // 16)] for u in range(2)]
+        x_q = []
+        for u in range(2):
+            cols = slice(u * HALF, (u + 1) * HALF)
+            nc.vector.tensor_copy(x_grouped[:, cols, X4 - 1], planes[X4 - 1][:].indirect(half_offsets[u]))
+            x_q.append(quantize(x_grouped[:, cols, :].rearrange("p n t -> p (n t)"), HALF, f"x{u}"))
+
+        h_grouped = [keep.tile([P, HALF, X4], BF16, name=f"h_grouped{u}", align_bytes=64) for u in range(2)]
+        h_q = []
+        y_banks = [psum.tile([P, G], F32, name=f"y_bank{t}") for t in range(X4)]
+        for u in range(2):
+            for c in range(HALF // CHUNK):
+                cols = slice(c * CHUNK, (c + 1) * CHUNK)
+                bank = psum.tile([P, X4, CHUNK], F32, name=f"a_bank{u}{c}")
+                for t in range(X4):
+                    rows = slice(t * P, (t + 1) * P)
+                    nc.tensor.matmul_mx(
+                        out=bank[:, t, :],
+                        lhsT=w1_q[0][:, rows].bitcast(FP8X4),
+                        lhsT_scale=w1_q[1][:, rows],
+                        rhs=x_q[u][0][:, cols].bitcast(FP8X4),
+                        rhs_scale=x_q[u][1][:, cols],
+                        start=True,
+                        stop=True,
+                    )
+                source = bank[:].rearrange("p t n -> p n t")
+                if (u, c) == (1, 1):
+                    nc.vector.tensor_scalar_max(h_grouped[u][:, cols, :], source, 0.0)
+                else:
+                    nc.scalar.activation(out=h_grouped[u][:, cols, :], in_=source, func=RELU)
+            h_q.append(quantize(h_grouped[u][:].rearrange("p n t -> p (n t)"), HALF, f"h{u}"))
+            for t in range(X4):
+                rows = slice(t * P, (t + 1) * P)
+                nc.tensor.matmul_mx(
+                    out=y_banks[t][:, u * HALF : (u + 1) * HALF],
+                    lhsT=w2_q[0][:, rows].bitcast(FP8X4),
+                    lhsT_scale=w2_q[1][:, rows],
+                    rhs=h_q[u][0][:].bitcast(FP8X4),
+                    rhs_scale=h_q[u][1][:],
+                    start=True,
+                    stop=True,
+                )
+
+        for u in range(2):
+            cols = slice(u * HALF, (u + 1) * HALF)
+            nc.vector.tensor_copy(picked[:, X4 - 1, cols], planes[X4 - 1][:].indirect(half_offsets[u]))
+
+        sums = [keep.tile([P, G], F32, name=f"sum{t}") for t in range(X4)]
+
+        def add(t):
+            nc.vector.tensor_tensor(out=sums[t][:], in0=y_banks[t][:], in1=picked[:, t, :], op=ADD)
+
+        add(0)
+        for t in range(X4):
+            if t + 1 < X4:
+                add(t + 1)
+            nc.vector.tensor_copy(planes[t][:].indirect(offsets[:]), sums[t][:])
+            nc.sync.dma_start(out=out_rows[t], in_=planes[t][:])

@@ -34,26 +34,12 @@ def tile_attend_mod_relu_kernel(tc, xT, w1, w2, offs, out):
         x_rows = xT.rearrange("(p t) n -> t p n", t=X4)
         out_rows = out.rearrange("(p t) n -> t p n", t=X4)
 
-        w1_raw = keep.tile([P, X4, H], F32, name="w1_raw")
-        w2_raw = keep.tile([P, X4, D], F32, name="w2_raw")
+        w_raw = [keep.tile([P, X4, 512], F32, name=f"w{i + 1}_raw") for i in range(2)]
         planes = [keep.tile([P, T], F32, name=f"plane{t}") for t in range(X4)]
-
-        nc.sync.dma_start(out=w1_raw[:], in_=w1.rearrange("(p j) c -> p j c", j=X4))
-        nc.sync.dma_start(out=planes[0][:], in_=x_rows[0])
-        nc.sync.dma_start(out=w2_raw[:], in_=w2.rearrange("(p j) c -> p j c", j=X4))
-        for t in range(1, X4):
+        for t in range(X4):
             nc.sync.dma_start(out=planes[t][:], in_=x_rows[t])
-
-        picked = keep.tile([P, X4, G], F32, name="picked")
-        x_grouped = keep.tile([P, G, X4], BF16, name="x_grouped", align_bytes=64)
-
-        def group_weights(raw, name):
-            grouped = keep.tile([P, X4 * 512], BF16, name=name + "_grouped", align_bytes=64)
-            nc.scalar.copy(
-                out=grouped[:].rearrange("p (t m j) -> p t m j", t=X4, j=X4),
-                in_=raw[:].rearrange("p j (m t) -> p t m j", t=X4),
-            )
-            return grouped
+        for i, w in enumerate((w1, w2)):
+            nc.sync.dma_start(out=w_raw[i][:], in_=w.rearrange("(p j) c -> p j c", j=X4))
 
         def quantize(grouped, width, name):
             codes = keep.tile([P, width], U32, name=name + "_codes", align_bytes=64)
@@ -61,73 +47,98 @@ def tile_attend_mod_relu_kernel(tc, xT, w1, w2, offs, out):
             nc.vector.quantize_mx(out=codes[:].bitcast(FP8X4), scales=scales[:], in_=grouped)
             return codes, scales
 
-        def early_plane(t):
-            nc.vector.tensor_copy(picked[:, t, :], planes[t][:].indirect(offsets[:]))
-            nc.vector.tensor_copy(x_grouped[:, :, t], picked[:, t, :])
+        def matmul(out_cols, weights, rows, moving, cols):
+            nc.tensor.matmul_mx(
+                out=out_cols,
+                lhsT=weights[0][:, rows].bitcast(FP8X4),
+                lhsT_scale=weights[1][:, rows],
+                rhs=moving[0][:, cols].bitcast(FP8X4),
+                rhs_scale=moving[1][:, cols],
+                start=True,
+                stop=True,
+            )
 
-        w1_grouped = group_weights(w1_raw, "w1")
-        early_plane(0)
-        w1_q = quantize(w1_grouped[:], H, "w1")
-        w2_grouped = group_weights(w2_raw, "w2")
-        early_plane(1)
-        early_plane(2)
-        w2_q = quantize(w2_grouped[:], D, "w2")
-
+        halves = [slice(u * HALF, (u + 1) * HALF) for u in range(2)]
         half_offsets = [offsets[:, u * (HALF // 16) : (u + 1) * (HALF // 16)] for u in range(2)]
-        x_q = []
-        for u in range(2):
-            cols = slice(u * HALF, (u + 1) * HALF)
-            nc.vector.tensor_copy(x_grouped[:, cols, X4 - 1], planes[X4 - 1][:].indirect(half_offsets[u]))
-            x_q.append(quantize(x_grouped[:, cols, :].rearrange("p n t -> p (n t)"), HALF, f"x{u}"))
+        picked = keep.tile([P, X4, G], F32, name="picked")
+        x_grouped = [keep.tile([P, HALF, X4], BF16, name=f"x_grouped{u}", align_bytes=64) for u in range(2)]
 
-        h_grouped = [keep.tile([P, HALF, X4], BF16, name=f"h_grouped{u}", align_bytes=64) for u in range(2)]
-        h_q = []
+        def group_pair(u, t):
+            nc.scalar.copy(
+                out=x_grouped[u][:, :, t : t + 2],
+                in_=picked[:, t : t + 2, halves[u]].rearrange("p t n -> p n t"),
+            )
+
+        for t in range(X4 - 1):
+            nc.vector.tensor_copy(picked[:, t, :], planes[t][:].indirect(offsets[:]))
+        for u in range(2):
+            group_pair(u, 0)
+        for u in range(2):
+            nc.vector.tensor_copy(picked[:, 3, halves[u]], planes[3][:].indirect(half_offsets[u]))
+            group_pair(u, 2)
+        x_q = [quantize(x_grouped[u][:].rearrange("p n t -> p (n t)"), HALF, f"x{u}") for u in range(2)]
+
+        w_grouped = [keep.tile([P, X4 * 512], BF16, name=f"w{i + 1}_grouped", align_bytes=64) for i in range(2)]
+
+        def group_weights(engine_copy, i, ms):
+            engine_copy(
+                w_grouped[i][:].rearrange("p (t m j) -> p m j t", t=X4, j=X4)[:, ms, :, :],
+                w_raw[i][:].rearrange("p j (m t) -> p m j t", t=X4)[:, ms, :, :],
+            )
+
+        group_weights(nc.vector.tensor_copy, 0, slice(48, P))
+        group_weights(nc.scalar.copy, 0, slice(0, 48))
+        w1_q = quantize(w_grouped[0][:], H, "w1")
+        group_weights(nc.vector.tensor_copy, 1, slice(32, P))
+        group_weights(nc.scalar.copy, 1, slice(0, 32))
+        w2_q = [
+            quantize(w_grouped[1][:, i * (2048 // 2) : (i + 1) * (2048 // 2)], D // 2, f"w2{i}")
+            for i in range(2)
+        ]
+
         y_banks = [psum.tile([P, G], F32, name=f"y_bank{t}") for t in range(X4)]
         for u in range(2):
+            h_grouped = keep.tile([P, HALF, X4], BF16, name=f"h_grouped{u}", align_bytes=64)
             for c in range(HALF // CHUNK):
                 cols = slice(c * CHUNK, (c + 1) * CHUNK)
                 bank = psum.tile([P, X4, CHUNK], F32, name=f"a_bank{u}{c}")
                 for t in range(X4):
-                    rows = slice(t * P, (t + 1) * P)
-                    nc.tensor.matmul_mx(
-                        out=bank[:, t, :],
-                        lhsT=w1_q[0][:, rows].bitcast(FP8X4),
-                        lhsT_scale=w1_q[1][:, rows],
-                        rhs=x_q[u][0][:, cols].bitcast(FP8X4),
-                        rhs_scale=x_q[u][1][:, cols],
-                        start=True,
-                        stop=True,
-                    )
-                source = bank[:].rearrange("p t n -> p n t")
-                if (u, c) == (1, 1):
-                    nc.vector.tensor_scalar_max(h_grouped[u][:, cols, :], source, 0.0)
-                else:
-                    nc.scalar.activation(out=h_grouped[u][:, cols, :], in_=source, func=RELU)
-            h_q.append(quantize(h_grouped[u][:].rearrange("p n t -> p (n t)"), HALF, f"h{u}"))
-            for t in range(X4):
-                rows = slice(t * P, (t + 1) * P)
-                nc.tensor.matmul_mx(
-                    out=y_banks[t][:, u * HALF : (u + 1) * HALF],
-                    lhsT=w2_q[0][:, rows].bitcast(FP8X4),
-                    lhsT_scale=w2_q[1][:, rows],
-                    rhs=h_q[u][0][:].bitcast(FP8X4),
-                    rhs_scale=h_q[u][1][:],
-                    start=True,
-                    stop=True,
+                    matmul(bank[:, t, :], w1_q, slice(t * P, (t + 1) * P), x_q[u], cols)
+                nc.scalar.activation(
+                    out=h_grouped[:, cols, :], in_=bank[:].rearrange("p t n -> p n t"), func=RELU
                 )
-
-        for u in range(2):
-            cols = slice(u * HALF, (u + 1) * HALF)
-            nc.vector.tensor_copy(picked[:, X4 - 1, cols], planes[X4 - 1][:].indirect(half_offsets[u]))
+            h_q = quantize(h_grouped[:].rearrange("p n t -> p (n t)"), HALF, f"h{u}")
+            for t in range(X4):
+                per = X4 // 2
+                rows = slice(t % per * P, (t % per + 1) * P)
+                matmul(y_banks[t][:, halves[u]], w2_q[t // per], rows, h_q, slice(0, HALF))
 
         sums = [keep.tile([P, G], F32, name=f"sum{t}") for t in range(X4)]
 
-        def add(t):
-            nc.vector.tensor_tensor(out=sums[t][:], in0=y_banks[t][:], in1=picked[:, t, :], op=ADD)
+        def add(t, cols):
+            nc.vector.tensor_tensor(out=sums[t][:, cols], in0=y_banks[t][:, cols], in1=picked[:, t, cols], op=ADD)
 
-        add(0)
-        for t in range(X4):
-            if t + 1 < X4:
-                add(t + 1)
+        results = [keep.tile([P, G], F32, name=f"result{t}") for t in range(X4)]
+
+        def add_beside(t, cols):
+            nc.scalar.copy(out=results[t][:, cols], in_=y_banks[t][:, cols])
+            nc.gpsimd.tensor_tensor(out=sums[t][:, cols], in0=results[t][:, cols], in1=picked[:, t, cols], op=ADD)
+
+        def scatter(t, u):
+            nc.vector.tensor_copy(planes[t][:].indirect(half_offsets[u]), sums[t][:, halves[u]])
+
+        add(0, halves[0])
+        add_beside(1, halves[0])
+        scatter(0, 0)
+        add_beside(0, halves[1])
+        scatter(1, 0)
+        add_beside(1, halves[1])
+        scatter(0, 1)
+        nc.sync.dma_start(out=out_rows[0], in_=planes[0][:])
+        add_beside(2, slice(0, G))
+        scatter(1, 1)
+        nc.sync.dma_start(out=out_rows[1], in_=planes[1][:])
+        add_beside(3, slice(0, G))
+        for t in (2, 3):
             nc.vector.tensor_copy(planes[t][:].indirect(offsets[:]), sums[t][:])
             nc.sync.dma_start(out=out_rows[t], in_=planes[t][:])

@@ -1,4 +1,5 @@
 import concourse.mybir as mybir
+from concourse.masks import make_identity
 
 FLOPS = 2 * 2 * 512 * 512 * 512
 
@@ -41,6 +42,15 @@ def tile_attend_mod_relu_kernel(tc, xT, w1, w2, offs, out):
         for i, w in enumerate((w1, w2)):
             nc.sync.dma_start(out=w_raw[i][:], in_=w.rearrange("(p j) c -> p j c", j=X4))
 
+        identity = keep.tile([P, P], F32, name="identity")
+        make_identity(nc, identity[:])
+        y_banks = [psum.tile([P, G], F32, name=f"y_bank{t}") for t in range(X4)]
+        for j in range(4):
+            for b in range(X4):
+                nc.tensor.transpose(
+                    y_banks[j][:, b * P : (b + 1) * P], w_raw[0][:, j, b * P : (b + 1) * P], identity[:]
+                )
+
         def quantize(grouped, width, name):
             codes = keep.tile([P, width], U32, name=name + "_codes", align_bytes=64)
             scales = keep.tile([P, width], U8, name=name + "_scales", align_bytes=64)
@@ -63,20 +73,18 @@ def tile_attend_mod_relu_kernel(tc, xT, w1, w2, offs, out):
         picked = keep.tile([P, X4, G], F32, name="picked")
         x_grouped = [keep.tile([P, HALF, X4], BF16, name=f"x_grouped{u}", align_bytes=64) for u in range(2)]
 
-        def group_pair(u, t):
-            nc.scalar.copy(
-                out=x_grouped[u][:, :, t : t + 2],
-                in_=picked[:, t : t + 2, halves[u]].rearrange("p t n -> p n t"),
-            )
-
         for t in range(X4 - 1):
             nc.vector.tensor_copy(picked[:, t, :], planes[t][:].indirect(offsets[:]))
         for u in range(2):
-            group_pair(u, 0)
+            nc.scalar.copy(
+                out=x_grouped[u][:, :, 0:2],
+                in_=picked[:, 0:2, halves[u]].rearrange("p t n -> p n t"),
+            )
+            nc.vector.tensor_copy(x_grouped[u][:, :, 2], picked[:, 2, halves[u]])
         for u in range(2):
             nc.vector.tensor_copy(picked[:, 3, halves[u]], planes[3][:].indirect(half_offsets[u]))
-            group_pair(u, 2)
-        x_q = [quantize(x_grouped[u][:].rearrange("p n t -> p (n t)"), HALF, f"x{u}") for u in range(2)]
+            nc.vector.tensor_copy(x_grouped[u][:, :, 3], picked[:, 3, halves[u]])
+        x_q = [quantize(x_grouped[0][:].rearrange("p n t -> p (n t)"), HALF, "x0")]
 
         w_grouped = [keep.tile([P, X4 * 512], BF16, name=f"w{i + 1}_grouped", align_bytes=64) for i in range(2)]
 
@@ -88,30 +96,17 @@ def tile_attend_mod_relu_kernel(tc, xT, w1, w2, offs, out):
 
         group_weights(nc.vector.tensor_copy, 0, slice(48, P))
         group_weights(nc.scalar.copy, 0, slice(0, 48))
-        w1_q = quantize(w_grouped[0][:], H, "w1")
-        group_weights(nc.vector.tensor_copy, 1, slice(32, P))
-        group_weights(nc.scalar.copy, 1, slice(0, 32))
+        w1_q = [
+            quantize(w_grouped[0][:, i * (2048 // 2) : (i + 1) * (2048 // 2)], H // 2, f"w1{i}")
+            for i in range(2)
+        ]
+        x_q.append(quantize(x_grouped[1][:].rearrange("p n t -> p (n t)"), HALF, "x1"))
+        group_weights(nc.vector.tensor_copy, 1, slice(40, P))
+        group_weights(nc.scalar.copy, 1, slice(0, 40))
         w2_q = [
             quantize(w_grouped[1][:, i * (2048 // 2) : (i + 1) * (2048 // 2)], D // 2, f"w2{i}")
             for i in range(2)
         ]
-
-        y_banks = [psum.tile([P, G], F32, name=f"y_bank{t}") for t in range(X4)]
-        for u in range(2):
-            h_grouped = keep.tile([P, HALF, X4], BF16, name=f"h_grouped{u}", align_bytes=64)
-            for c in range(HALF // CHUNK):
-                cols = slice(c * CHUNK, (c + 1) * CHUNK)
-                bank = psum.tile([P, X4, CHUNK], F32, name=f"a_bank{u}{c}")
-                for t in range(X4):
-                    matmul(bank[:, t, :], w1_q, slice(t * P, (t + 1) * P), x_q[u], cols)
-                nc.scalar.activation(
-                    out=h_grouped[:, cols, :], in_=bank[:].rearrange("p t n -> p n t"), func=RELU
-                )
-            h_q = quantize(h_grouped[:].rearrange("p n t -> p (n t)"), HALF, f"h{u}")
-            for t in range(X4):
-                per = X4 // 2
-                rows = slice(t % per * P, (t % per + 1) * P)
-                matmul(y_banks[t][:, halves[u]], w2_q[t // per], rows, h_q, slice(0, HALF))
 
         sums = [keep.tile([P, G], F32, name=f"sum{t}") for t in range(X4)]
 
@@ -124,11 +119,28 @@ def tile_attend_mod_relu_kernel(tc, xT, w1, w2, offs, out):
             nc.scalar.copy(out=results[t][:, cols], in_=y_banks[t][:, cols])
             nc.gpsimd.tensor_tensor(out=sums[t][:, cols], in0=results[t][:, cols], in1=picked[:, t, cols], op=ADD)
 
+        for u in range(2):
+            h_grouped = keep.tile([P, HALF, X4], BF16, name=f"h_grouped{u}", align_bytes=64)
+            for c in range(HALF // CHUNK):
+                cols = slice(c * CHUNK, (c + 1) * CHUNK)
+                bank = psum.tile([P, X4, CHUNK], F32, name=f"a_bank{u}{c}")
+                for t in range(X4):
+                    matmul(bank[:, t, :], w1_q[t // 2], slice(t % 2 * P, (t % 2 + 1) * P), x_q[u], cols)
+                nc.scalar.activation(
+                    out=h_grouped[:, cols, :], in_=bank[:].rearrange("p t n -> p n t"), func=RELU
+                )
+            h_q = quantize(h_grouped[:].rearrange("p n t -> p (n t)"), HALF, f"h{u}")
+            for t in range(X4):
+                per = X4 // 2
+                rows = slice(t % per * P, (t % per + 1) * P)
+                matmul(y_banks[t][:, halves[u]], w2_q[t // per], rows, h_q, slice(0, HALF))
+            if u == 0:
+                add(0, halves[0])
+                add_beside(1, halves[0])
+
         def scatter(t, u):
             nc.vector.tensor_copy(planes[t][:].indirect(half_offsets[u]), sums[t][:, halves[u]])
 
-        add(0, halves[0])
-        add_beside(1, halves[0])
         scatter(0, 0)
         add_beside(0, halves[1])
         scatter(1, 0)

import concourse.mybir as mybir
from concourse.masks import make_identity

FLOPS = 2 * 2 * 512 * 512 * 512

F32 = mybir.dt.float32
BF16 = mybir.dt.bfloat16
U32 = mybir.dt.uint32
U16 = mybir.dt.uint16
U8 = mybir.dt.uint8
FP8X4 = mybir.dt.float8_e4m3fn_x4
ADD = mybir.AluOpType.add
RELU = mybir.ActivationFunctionType.Relu

P = 128
T = 2048
D = 512
H = 512
G = 512
X4 = 4
HALF = G // 2
CHUNK = 128


def tile_attend_mod_relu_kernel(tc, xT, w1, w2, offs, out):
    nc = tc.nc
    with (
        tc.tile_pool(name="lists", bufs=1) as lists,
        tc.tile_pool(name="keep", bufs=1) as keep,
        tc.psum_pool(name="psum", bufs=1) as psum,
    ):
        offsets = lists.tile([P, G // 16], U16, name="offsets")
        nc.sync.dma_start(offsets[:], offs)

        x_rows = xT.rearrange("(p t) n -> t p n", t=X4)
        out_rows = out.rearrange("(p t) n -> t p n", t=X4)

        w_raw = [keep.tile([P, X4, 512], F32, name=f"w{i + 1}_raw") for i in range(2)]
        planes = [keep.tile([P, T], F32, name=f"plane{t}") for t in range(X4)]
        for t in range(X4):
            nc.sync.dma_start(out=planes[t][:], in_=x_rows[t])
        for i, w in enumerate((w1, w2)):
            nc.sync.dma_start(out=w_raw[i][:], in_=w.rearrange("(p j) c -> p j c", j=X4))

        identity = keep.tile([P, P], F32, name="identity")
        make_identity(nc, identity[:])
        y_banks = [psum.tile([P, G], F32, name=f"y_bank{t}") for t in range(X4)]
        for j in range(4):
            for b in range(X4):
                nc.tensor.transpose(
                    y_banks[j][:, b * P : (b + 1) * P], w_raw[0][:, j, b * P : (b + 1) * P], identity[:]
                )

        def quantize(grouped, width, name):
            codes = keep.tile([P, width], U32, name=name + "_codes", align_bytes=64)
            scales = keep.tile([P, width], U8, name=name + "_scales", align_bytes=64)
            nc.vector.quantize_mx(out=codes[:].bitcast(FP8X4), scales=scales[:], in_=grouped)
            return codes, scales

        def matmul(out_cols, weights, rows, moving, cols):
            nc.tensor.matmul_mx(
                out=out_cols,
                lhsT=weights[0][:, rows].bitcast(FP8X4),
                lhsT_scale=weights[1][:, rows],
                rhs=moving[0][:, cols].bitcast(FP8X4),
                rhs_scale=moving[1][:, cols],
                start=True,
                stop=True,
            )

        halves = [slice(u * HALF, (u + 1) * HALF) for u in range(2)]
        half_offsets = [offsets[:, u * (HALF // 16) : (u + 1) * (HALF // 16)] for u in range(2)]
        picked = keep.tile([P, X4, G], F32, name="picked")
        x_grouped = [keep.tile([P, HALF, X4], BF16, name=f"x_grouped{u}", align_bytes=64) for u in range(2)]

        for t in range(X4 - 1):
            nc.vector.tensor_copy(picked[:, t, :], planes[t][:].indirect(offsets[:]))
        for u in range(2):
            nc.scalar.copy(
                out=x_grouped[u][:, :, 0:2],
                in_=picked[:, 0:2, halves[u]].rearrange("p t n -> p n t"),
            )
            nc.vector.tensor_copy(x_grouped[u][:, :, 2], picked[:, 2, halves[u]])
        for u in range(2):
            nc.vector.tensor_copy(picked[:, 3, halves[u]], planes[3][:].indirect(half_offsets[u]))
            nc.vector.tensor_copy(x_grouped[u][:, :, 3], picked[:, 3, halves[u]])
        x_q = [quantize(x_grouped[0][:].rearrange("p n t -> p (n t)"), HALF, "x0")]

        w_grouped = [keep.tile([P, X4 * 512], BF16, name=f"w{i + 1}_grouped", align_bytes=64) for i in range(2)]

        def group_weights(engine_copy, i, ms):
            engine_copy(
                w_grouped[i][:].rearrange("p (t m j) -> p m j t", t=X4, j=X4)[:, ms, :, :],
                w_raw[i][:].rearrange("p j (m t) -> p m j t", t=X4)[:, ms, :, :],
            )

        group_weights(nc.vector.tensor_copy, 0, slice(48, P))
        group_weights(nc.scalar.copy, 0, slice(0, 48))
        w1_q = [
            quantize(w_grouped[0][:, i * (2048 // 2) : (i + 1) * (2048 // 2)], H // 2, f"w1{i}")
            for i in range(2)
        ]
        x_q.append(quantize(x_grouped[1][:].rearrange("p n t -> p (n t)"), HALF, "x1"))
        group_weights(nc.vector.tensor_copy, 1, slice(40, P))
        group_weights(nc.scalar.copy, 1, slice(0, 40))
        w2_q = [
            quantize(w_grouped[1][:, i * (2048 // 2) : (i + 1) * (2048 // 2)], D // 2, f"w2{i}")
            for i in range(2)
        ]

        sums = [keep.tile([P, G], F32, name=f"sum{t}") for t in range(X4)]

        def add(t, cols):
            nc.vector.tensor_tensor(out=sums[t][:, cols], in0=y_banks[t][:, cols], in1=picked[:, t, cols], op=ADD)

        results = [keep.tile([P, G], F32, name=f"result{t}") for t in range(X4)]

        def add_beside(t, cols):
            nc.scalar.copy(out=results[t][:, cols], in_=y_banks[t][:, cols])
            nc.gpsimd.tensor_tensor(out=sums[t][:, cols], in0=results[t][:, cols], in1=picked[:, t, cols], op=ADD)

        for u in range(2):
            h_grouped = keep.tile([P, HALF, X4], BF16, name=f"h_grouped{u}", align_bytes=64)
            for c in range(HALF // CHUNK):
                cols = slice(c * CHUNK, (c + 1) * CHUNK)
                bank = psum.tile([P, X4, CHUNK], F32, name=f"a_bank{u}{c}")
                for t in range(X4):
                    matmul(bank[:, t, :], w1_q[t // 2], slice(t % 2 * P, (t % 2 + 1) * P), x_q[u], cols)
                nc.scalar.activation(
                    out=h_grouped[:, cols, :], in_=bank[:].rearrange("p t n -> p n t"), func=RELU
                )
            h_q = quantize(h_grouped[:].rearrange("p n t -> p (n t)"), HALF, f"h{u}")
            for t in range(X4):
                per = X4 // 2
                rows = slice(t % per * P, (t % per + 1) * P)
                matmul(y_banks[t][:, halves[u]], w2_q[t // per], rows, h_q, slice(0, HALF))
            if u == 0:
                add(0, halves[0])
                add_beside(1, halves[0])

        def scatter(t, u):
            nc.vector.tensor_copy(planes[t][:].indirect(half_offsets[u]), sums[t][:, halves[u]])

        scatter(0, 0)
        add_beside(0, halves[1])
        scatter(1, 0)
        add_beside(1, halves[1])
        scatter(0, 1)
        nc.sync.dma_start(out=out_rows[0], in_=planes[0][:])
        add_beside(2, slice(0, G))
        scatter(1, 1)
        nc.sync.dma_start(out=out_rows[1], in_=planes[1][:])
        add_beside(3, slice(0, G))
        for t in (2, 3):
            nc.vector.tensor_copy(planes[t][:].indirect(offsets[:]), sums[t][:])
            nc.sync.dma_start(out=out_rows[t], in_=planes[t][:])
